import numpy as np
import ml_dtypes


def mxq(x, axis, fmt="e4m3"):
    dtype, down = {"e4m3": (ml_dtypes.float8_e4m3fn, 7), "e5m2": (ml_dtypes.float8_e5m2, 14)}[fmt]
    v = np.moveaxis(np.asarray(x, np.float32).astype(ml_dtypes.bfloat16).astype(np.float64), axis, -1)
    blocks = v.reshape(v.shape[:-1] + (-1, 32))
    amax = np.abs(blocks).max(-1, keepdims=True)
    byte = np.maximum(np.where(amax > 0, np.frexp(amax)[1] - 1 + 127, 0) - down, 1)
    scale = np.exp2(byte - 127.0)
    codes = (blocks / scale).astype(np.float32).astype(dtype).astype(np.float64)
    return np.moveaxis((codes * scale).reshape(v.shape), -1, axis)


WIDE = False


def mx_kscale(k):
    if not WIDE:
        return np.ones(k)
    levels = np.array([10, -10, 5, -5, 0])
    if k % 512:
        return np.exp2(np.random.permutation(np.resize(levels, k // 32))).repeat(32)
    a = np.empty((k // 512, 16))
    for p in range(k // 512):
        a[p, :8] = np.random.permutation(np.resize(levels, 8))
        for g in range(8):
            far = levels[np.abs(levels - a[p, g]) >= 10]
            a[p, g + 8] = far[np.random.randint(len(far))]
    return np.exp2(a.ravel()).repeat(32)


def f64(x):
    return np.asarray(x).astype(np.float64)


def striped(idx):
    return np.tile(np.asarray(idx).reshape(-1, 16).T, (8, 1)).astype(np.uint16)


def unstriped(offs):
    return offs[:16].T.reshape(-1).astype(np.int64)


E2M1 = np.array([0.0, 0.5, 1.0, 1.5, 2.0, 3.0, 4.0, 6.0, -0.0, -0.5, -1.0, -1.5, -2.0, -3.0, -4.0, -6.0])


def pack_weight(w, fmt):
    k, n = w.shape
    w = f64(np.asarray(w, np.float32).astype(ml_dtypes.bfloat16)).reshape(k // 32, 32, n)
    amax = np.abs(w).max(1)
    if fmt == "e4m3":
        byte = np.frexp(amax)[1] - 1 + 127 - 7
    else:
        mant, ex = np.frexp(amax / 6.0)
        byte = np.where(mant > 0.5, ex, ex - 1) + 127
    byte = np.clip(np.where(amax > 0, byte, 1), 1, 254)
    scaled = (w * np.exp2(127.0 - byte)[:, None, :]).reshape(k, n).astype(np.float32)
    by_word = np.ascontiguousarray(scaled.reshape(k // 512, 128, 4, n).transpose(0, 1, 3, 2))
    if fmt == "e4m3":
        words = by_word.astype(ml_dtypes.float8_e4m3fn).view(np.uint8)
    else:
        c = by_word.astype(ml_dtypes.float4_e2m1fn).view(np.uint8) & 0xF
        words = (c[..., 0::2] | (c[..., 1::2] << 4)).reshape(k // 512, 128, 2 * n)
    return np.ascontiguousarray(words), np.ascontiguousarray(byte.astype(np.uint8).reshape(k // 512, 16, n))


def unpack_weight(words, scales, fmt):
    g, _, n = scales.shape
    words = np.ascontiguousarray(words).reshape(g, 128, n, -1)
    if fmt == "e4m3":
        vals = words.view(ml_dtypes.float8_e4m3fn).astype(np.float64)
    else:
        nib = np.empty((g, 128, n, 4), np.uint8)
        nib[..., 0::2] = words & 0xF
        nib[..., 1::2] = words >> 4
        vals = E2M1[nib]
    vals = vals * np.repeat(np.exp2(scales.astype(np.float64) - 127.0), 8, axis=1)[..., None]
    return vals.transpose(0, 1, 3, 2).reshape(g * 512, n)


B, N, T, D, DV, NQ = 2, 512, 2048, 1024, 128, 128


def setup_inputs():
    n = np.random.standard_normal
    seg = T // B
    idx = np.concatenate([b * seg + np.random.permutation(seg)[:N] for b in range(B)])
    s = mx_kscale(D)[:, None]
    u = np.ones(T)
    u[idx] = mx_kscale(B * N)
    r = np.random.uniform(0.5, 2.0, T)
    k = n((D, T)) / s
    v = n((DV, T)) / (u * r)
    kp = pack_weight(k, "e2m1")
    return {
        "qT": (n((B, D, NQ)) * s * (0.80 / np.sqrt(D))).astype(np.float32),
        "k_words": np.ascontiguousarray(kp[0].reshape(D // 1024, 2, 128, T, 2).transpose(0, 2, 3, 1, 4)).reshape(D // 1024, 128, T, 4),
        "k_scales": kp[1],
        "vT": v.astype(np.float32),
        "vs": np.tile(u * r, (128, 1)).astype(np.float32),
        "kb": np.tile(n(T), (128, 1)).astype(np.float32),
        "offs": striped(idx),
    }


def reference(qT, k_words, k_scales, vT, vs, kb, offs):
    idx = unstriped(offs)
    k = unpack_weight(k_words.reshape(D // 1024, 128, T, 2, 2).transpose(0, 3, 1, 2, 4).reshape(D // 512, 128, 2 * T), k_scales, "e2m1")
    v = f64(vT)
    pick = lambda x: x[:, idx].reshape(x.shape[0], B, N).transpose(1, 0, 2)
    q = f64(qT)
    score = mxq(q, 1, "e4m3").transpose(0, 2, 1) @ pick(k)
    score = score + pick(f64(kb))[:, :1, :]
    p = np.square(np.maximum(score, 0.0))
    total = p.sum(-1, keepdims=True) + 1.0
    w = p * pick(f64(vs))[:, :1, :]
    y = mxq(w, 2, "e4m3") @ mxq(pick(v).transpose(0, 2, 1), 1, "e4m3")
    y = y / total
    return y

@@ -1,0 +1,228 @@
+from contextlib import ExitStack
+
+import concourse.mybir as mybir
+from concourse.masks import make_identity
+
+B, N, T, D, DV, NQ = 2, 512, 2048, 1024, 128, 128
+SEG = T // B
+P = 128
+PACK = 4
+PASSES = D // (P * PACK)
+
+FLOPS = 2 * B * NQ * N * (D + DV)
+BYTES = 4 * B * D * NQ + 4 * P * T + PASSES * 16 * T + 4 * DV * T + 2 * 4 * T + 2 * P * (B * N // 16) + 4 * B * NQ * DV
+
+F32 = mybir.dt.float32
+BF16 = mybir.dt.bfloat16
+I32 = mybir.dt.int32
+U32 = mybir.dt.uint32
+U16 = mybir.dt.uint16
+U8 = mybir.dt.uint8
+FP8X4 = mybir.dt.float8_e4m3fn_x4
+FP4X4 = mybir.dt.float4_e2m1fn_x4
+ACT = mybir.ActivationFunctionType
+ALU = mybir.AluOpType
+
+ROW = P - 1
+FREE = 24
+SPAN = 100
+
+
+def tile_attend_rel2_kb_segb2q128n512t2048_kernel(tc, qT, k_words, k_scales, vT, vs, kb, offs, out):
+    nc = tc.nc
+    with ExitStack() as ctx:
+        lists = ctx.enter_context(tc.tile_pool(name="lists", bufs=1))
+        sb = ctx.enter_context(tc.tile_pool(name="sb", bufs=1))
+        ps = ctx.enter_context(tc.psum_pool(name="ps", bufs=1))
+
+        def tile(name, shape, dtype, tag=""):
+            return sb.tile(shape, dtype, name=name, tag=tag or name, align_bytes=64)
+
+        offsets = lists.tile([P, B * N // 16], U16, name="offsets")
+        seq_offsets = [offsets[:, b * N // 16 : (b + 1) * N // 16] for b in range(B)]
+
+        scale_pool = tile("scale_pool", [P, T], U8)
+        kb_pool = tile("kb_pool", [P, T], F32)
+        vs_pool = tile("vs_pool", [P, T], F32)
+        word_pool = tile("word_pool", [P, T], I32)
+        v_pool = [tile("v_pool0", [P, SEG], F32)]
+        q_raw = [tile("q_raw%d" % b, [P, PASSES, PACK, NQ], F32) for b in range(B)]
+        k_scale_slot = tile("k_scale_slot", [P, B * N], U8)
+        k_scale = tile("k_scale", [P, PASSES * B * N], U8)
+        ident = tile("ident", [P, P], F32)
+
+        nc.sync.dma_start(offsets[:], offs)
+        nc.sync.dma_start(kb_pool[ROW:P, :], kb[0:1, :])
+        for quad in range(4):
+            nc.sync.dma_start(
+                scale_pool[32 * quad + FREE : 32 * quad + 32, :].bitcast(I32),
+                k_scales[:, 4 * quad : 4 * quad + 4, :].bitcast(I32),
+            )
+        words_hbm = k_words[0].rearrange("p t c -> p (t c)").bitcast(I32)
+
+        def load_keys(b):
+            nc.sync.dma_start(word_pool[:, b * SEG : (b + 1) * SEG], words_hbm[:, b * SEG : (b + 1) * SEG])
+
+        def load_queries(b):
+            nc.sync.dma_start(q_raw[b][:], qT[b].rearrange("(o p j) q -> p o j q", o=PASSES, j=PACK))
+
+        load_keys(0)
+        load_queries(0)
+        nc.sync.dma_start(vs_pool[ROW:P, :], vs[0:1, :])
+        load_keys(1)
+        load_queries(1)
+        nc.sync.dma_start(v_pool[0][:], vT[:, 0:SEG])
+
+        for quad in range(4):
+            nc.gpsimd.memset(scale_pool[32 * quad : 32 * quad + FREE, :].bitcast(I32), 0)
+        nc.vector.memset(kb_pool[0:ROW, 0 : SEG - 1], 0.0)
+        nc.vector.memset(kb_pool[0:ROW, SEG - 1 : T], 0.0)
+        nc.gpsimd.memset(k_scale[96:P, :].bitcast(I32), 0)
+        nc.gpsimd.memset(vs_pool[0:ROW, :], 0.0)
+        make_identity(nc, ident[:])
+
+        nc.vector.tensor_copy(
+            k_scale_slot[:].rearrange("p (r n) -> p n r", r=PACK),
+            scale_pool[:].indirect(offsets[:]),
+        )
+        for o in range(PASSES):
+            nc.sync.dma_start(
+                k_scale[0:SPAN, o * B * N : (o + 1) * B * N].bitcast(I32),
+                k_scale_slot[FREE + 4 * o : FREE + 4 * o + SPAN, :].bitcast(I32),
+            )
+        v_pool.append(tile("v_pool1", [P, T], F32, tag="scale_pool"))
+        nc.sync.dma_start(v_pool[1][:, SEG:T], vT[:, SEG:T])
+
+        def token_columns(name, pool, b):
+            row = tile("%s_row%d" % (name, b), [P, N], F32)
+            col = tile("%s_col%d" % (name, b), [P, PACK], F32)
+            nc.scalar.activation(row[:], pool[:].indirect(seq_offsets[b]), ACT.Copy)
+            nc.scalar.dma_start(col[:], row[ROW:P, :].rearrange("p (s r) -> p s r", r=PACK))
+            return col
+
+        kb_col = [token_columns("kb", kb_pool, b) for b in range(B)]
+        vs_col = [token_columns("vs", vs_pool, b) for b in range(B)]
+
+        banks = [[ps.tile([P, 4, NQ], F32, name="scores%d%d" % (b, h)) for h in range(2)] for b in range(B)]
+        scores = [[banks[b][r // 2][:, r % 2, :] for r in range(PACK)] for b in range(B)]
+        v_turn = [banks[0][b][:, 2:4, :] for b in range(B)]
+        tail = [ps.tile([P, 2, P], F32, name="tail%d" % b) for b in range(B)]
+
+        k_pair = [tile("k_pair%d" % b, [P, N], U32) for b in range(B)]
+        k_code = [tile("k_code%d" % b, [P, PASSES * N * 2], U8) for b in range(B)]
+        q_bf = [tile("q_bf%d" % b, [P, PASSES * NQ * PACK], BF16) for b in range(B)]
+        q_code = [tile("q_code%d" % b, [P, PASSES * NQ], U32) for b in range(B)]
+        q_scale = [tile("q_scale%d" % b, [P, PASSES * NQ], U8) for b in range(B)]
+
+        def keys_and_scores(b):
+            nc.vector.tensor_copy(
+                k_pair[b][:].rearrange("p (r s) -> p s r", r=PACK),
+                word_pool[:, 0 : (b + 1) * SEG].bitcast(U32).indirect(seq_offsets[b]),
+            )
+            nc.gpsimd.tensor_scalar(
+                q_bf[b][:].rearrange("p (o q j) -> p o q j", o=PASSES, j=PACK),
+                q_raw[b][:].rearrange("p o j q -> p o q j"),
+                1.0,
+                0.0,
+                ALU.mult,
+                ALU.add,
+            )
+            nc.vector.tensor_copy(
+                k_code[b][:].bitcast(U16).rearrange("p (o n) -> p o n", o=PASSES),
+                k_pair[b][:].bitcast(U16).rearrange("p (n o) -> p o n", o=PASSES),
+            )
+            nc.vector.quantize_mx(out=q_code[b][:].bitcast(FP8X4), scales=q_scale[b][:], in_=q_bf[b][:])
+            for r in range(PACK):
+                for o in range(PASSES):
+                    at = (o * N + r * P) * 2
+                    col = o * B * N + (r * B + b) * P
+                    nc.tensor.matmul_mx(
+                        out=scores[b][r],
+                        lhsT=k_code[b][:, at : at + 2 * P].bitcast(FP4X4),
+                        lhsT_scale=k_scale[:, col : col + P],
+                        rhs=q_code[b][:, o * NQ : (o + 1) * NQ].bitcast(FP8X4),
+                        rhs_scale=q_scale[b][:, o * NQ : (o + 1) * NQ],
+                        start=(o == 0),
+                        stop=(o == PASSES - 1),
+                    )
+
+        v_bf = [tile("v_bf%d" % b, [P, DV * PACK], BF16) for b in range(B)]
+        v_code = [tile("v_code%d" % b, [P, DV], U32) for b in range(B)]
+        v_scale = [tile("v_scale%d" % b, [P, DV], U8) for b in range(B)]
+
+        def values(b):
+            v_slot = tile("v_slot%d" % b, [P, N], BF16, tag="relu0" if b else "")
+            if b == 0:
+                nc.vector.tensor_copy(v_slot[:], v_pool[b][:].indirect(seq_offsets[b]))
+            else:
+                nc.scalar.activation(v_slot[:], v_pool[b][:].indirect(seq_offsets[b]), ACT.Copy)
+            pairs = v_slot[:].bitcast(F32)
+            for u in range(2):
+                nc.tensor.transpose(v_turn[b][:, u, :], pairs[:, u : N // 2 : 2], ident[:])
+            nc.scalar.copy(
+                v_bf[b][:].bitcast(F32).rearrange("p (e u) -> p e u", u=2),
+                v_turn[b].rearrange("p u e -> p e u"),
+            )
+            nc.vector.quantize_mx(out=v_code[b][:].bitcast(FP8X4), scales=v_scale[b][:], in_=v_bf[b][:])
+
+        relu = [tile("relu%d" % b, [P, PACK, NQ], F32) for b in range(B)]
+        prob = [tile("prob%d" % b, [P, PACK, NQ], F32) for b in range(B)]
+        w_bf = [tile("w_bf%d" % b, [P, NQ * PACK], BF16) for b in range(B)]
+        w_code = [tile("w_code%d" % b, [P, NQ], U32) for b in range(B)]
+        w_scale = [tile("w_scale%d" % b, [P, NQ], U8) for b in range(B)]
+        part = [tile("part%d" % b, [P, P], F32) for b in range(B)]
+        total = [tile("total%d" % b, [P, 1], F32) for b in range(B)]
+        inv = [tile("inv%d" % b, [P, 1], F32) for b in range(B)]
+        res = [tile("res%d" % b, [P, DV], F32) for b in range(B)]
+
+        def positive_scores(b):
+            last = b == B - 1
+            for r in range(PACK):
+                score, bias = scores[b][r], kb_col[b][:, r : r + 1]
+                if last:
+                    nc.vector.tensor_scalar(relu[b][:, r, :], score, bias, 0.0, ALU.add, ALU.max)
+                else:
+                    nc.scalar.activation(relu[b][:, r, :], score, ACT.Relu, bias=bias)
+            nc.scalar.activation(prob[b][:], relu[b][:], ACT.Square)
+
+        def weights(b):
+            nc.vector.tensor_tensor(
+                w_bf[b][:].rearrange("p (q r) -> p q r", r=PACK),
+                prob[b][:].rearrange("p r q -> p q r"),
+                vs_col[b][:].unsqueeze(1).broadcast_to([P, NQ, PACK]),
+                ALU.mult,
+            )
+            for r in range(PACK):
+                nc.tensor.matmul(
+                    tail[b][:, 0, :], prob[b][:, r, :], ident[:], start=(r == 0), stop=(r == PACK - 1), is_transpose=True
+                )
+            nc.vector.tensor_scalar(
+                part[b][:], tail[b][:, 0, :], 1.0, 1.0, ALU.mult, ALU.add, accum_out=total[b][:]
+            )
+            nc.vector.quantize_mx(out=w_code[b][:].bitcast(FP8X4), scales=w_scale[b][:], in_=w_bf[b][:])
+            nc.vector.reciprocal(inv[b][:], total[b][:])
+
+        def finish(b):
+            nc.tensor.matmul_mx(
+                out=tail[b][:, 1, :],
+                lhsT=w_code[b][:].bitcast(FP8X4),
+                lhsT_scale=w_scale[b][:],
+                rhs=v_code[b][:].bitcast(FP8X4),
+                rhs_scale=v_scale[b][:],
+                start=True,
+                stop=True,
+            )
+            nc.scalar.activation(res[b][:], tail[b][:, 1, :], ACT.Copy, scale=inv[b][:])
+            nc.sync.dma_start(out[b], res[b][:])
+
+        keys_and_scores(0)
+        nc.gpsimd.memset(v_pool[1][:, 0:SEG], 0.0)
+        keys_and_scores(1)
+        positive_scores(0)
+        values(0)
+        positive_scores(1)
+        weights(0)
+        values(1)
+        finish(0)
+        weights(1)
+        finish(1)

@@ -24,8 +24,8 @@ ACT = mybir.ActivationFunctionType
 ALU = mybir.AluOpType
 
 ROW = P - 1
-FREE = 24
-SPAN = 100
+FREE = 16
+HALF = P // 2
 
 
 def tile_attend_rel2_kb_segb2q128n512t2048_kernel(tc, qT, k_words, k_scales, vT, vs, kb, offs, out):
@@ -45,7 +45,6 @@ def tile_attend_rel2_kb_segb2q128n512t2048_kernel(tc, qT, k_words, k_scales, vT,
         kb_pool = tile("kb_pool", [P, T], F32)
         vs_pool = tile("vs_pool", [P, T], F32)
         word_pool = tile("word_pool", [P, T], I32)
-        v_pool = [tile("v_pool0", [P, SEG], F32)]
         q_raw = [tile("q_raw%d" % b, [P, PASSES, PACK, NQ], F32) for b in range(B)]
         k_scale_slot = tile("k_scale_slot", [P, B * N], U8)
         k_scale = tile("k_scale", [P, PASSES * B * N], U8)
@@ -53,31 +52,27 @@ def tile_attend_rel2_kb_segb2q128n512t2048_kernel(tc, qT, k_words, k_scales, vT,
 
         nc.sync.dma_start(offsets[:], offs)
         nc.sync.dma_start(kb_pool[ROW:P, :], kb[0:1, :])
-        for quad in range(4):
+        scale_rows = k_scales.rearrange("o (h c j) t -> c (o h) j t", h=2, c=2)
+        for c in range(2):
             nc.sync.dma_start(
-                scale_pool[32 * quad + FREE : 32 * quad + 32, :].bitcast(I32),
-                k_scales[:, 4 * quad : 4 * quad + 4, :].bitcast(I32),
+                scale_pool[32 * c + FREE : 32 * c + 32, :].bitcast(I32),
+                scale_rows[c].bitcast(I32),
             )
         words_hbm = k_words[0].rearrange("p t c -> p (t c)").bitcast(I32)
 
-        def load_keys(b):
-            nc.sync.dma_start(word_pool[:, b * SEG : (b + 1) * SEG], words_hbm[:, b * SEG : (b + 1) * SEG])
 
         def load_queries(b):
             nc.sync.dma_start(q_raw[b][:], qT[b].rearrange("(o p j) q -> p o j q", o=PASSES, j=PACK))
 
-        load_keys(0)
         load_queries(0)
+        nc.sync.dma_start(word_pool[:], words_hbm)
         nc.sync.dma_start(vs_pool[ROW:P, :], vs[0:1, :])
-        load_keys(1)
         load_queries(1)
-        nc.sync.dma_start(v_pool[0][:], vT[:, 0:SEG])
 
-        for quad in range(4):
-            nc.gpsimd.memset(scale_pool[32 * quad : 32 * quad + FREE, :].bitcast(I32), 0)
+        for rows in (slice(0, FREE), slice(32, 32 + FREE), slice(HALF, P)):
+            nc.gpsimd.memset(scale_pool[rows, :].bitcast(I32), 0)
         nc.vector.memset(kb_pool[0:ROW, 0 : SEG - 1], 0.0)
         nc.vector.memset(kb_pool[0:ROW, SEG - 1 : T], 0.0)
-        nc.gpsimd.memset(k_scale[96:P, :].bitcast(I32), 0)
         nc.gpsimd.memset(vs_pool[0:ROW, :], 0.0)
         make_identity(nc, ident[:])
 
@@ -86,52 +81,66 @@ def tile_attend_rel2_kb_segb2q128n512t2048_kernel(tc, qT, k_words, k_scales, vT,
             scale_pool[:].indirect(offsets[:]),
         )
         for o in range(PASSES):
-            nc.sync.dma_start(
-                k_scale[0:SPAN, o * B * N : (o + 1) * B * N].bitcast(I32),
-                k_scale_slot[FREE + 4 * o : FREE + 4 * o + SPAN, :].bitcast(I32),
-            )
-        v_pool.append(tile("v_pool1", [P, T], F32, tag="scale_pool"))
-        nc.sync.dma_start(v_pool[1][:, SEG:T], vT[:, SEG:T])
+            for h in range(2):
+                first = FREE + 4 * (2 * o + h)
+                nc.sync.dma_start(
+                    k_scale[h * HALF : (h + 1) * HALF, o * B * N : (o + 1) * B * N].bitcast(I32),
+                    k_scale_slot[first : first + HALF, :].bitcast(I32),
+                )
+        v_pool = tile("v_pool", [P, T], F32, tag="scale_pool")
+        nc.sync.dma_start(v_pool[:], vT)
 
-        def token_columns(name, pool, b):
+        def gather_row(name, pool, b):
             row = tile("%s_row%d" % (name, b), [P, N], F32)
-            col = tile("%s_col%d" % (name, b), [P, PACK], F32)
             nc.scalar.activation(row[:], pool[:].indirect(seq_offsets[b]), ACT.Copy)
-            nc.scalar.dma_start(col[:], row[ROW:P, :].rearrange("p (s r) -> p s r", r=PACK))
-            return col
+            return row
 
-        kb_col = [token_columns("kb", kb_pool, b) for b in range(B)]
-        vs_col = [token_columns("vs", vs_pool, b) for b in range(B)]
+        kb_row = [gather_row("kb", kb_pool, b) for b in range(B)]
+        vs_row = [gather_row("vs", vs_pool, b) for b in range(B)]
 
-        banks = [[ps.tile([P, 4, NQ], F32, name="scores%d%d" % (b, h)) for h in range(2)] for b in range(B)]
-        scores = [[banks[b][r // 2][:, r % 2, :] for r in range(PACK)] for b in range(B)]
-        v_turn = [banks[0][b][:, 2:4, :] for b in range(B)]
+        banks = [[ps.tile([P, 2, 2 * P], F32, name="scores%d%d" % (b, h)) for h in range(2)] for b in range(B)]
+        scores = [[banks[b][r // 2][:, 0, (r % 2) * NQ : (r % 2 + 1) * NQ] for r in range(PACK)] for b in range(B)]
+        kb_bank = ps.tile([P, 2, 2 * P], F32, name="kb_bank")
+        vs_bank = ps.tile([P, 2 * P], F32, name="vs_bank")
+        vs_turn = [vs_bank[:], banks[0][0][:, 1, :]]
+        v_turn = [area.rearrange("p (u e) -> p u e", u=2) for area in (banks[0][1][:, 1, :], kb_bank[:, 1, :])]
+
+        def turn_row(area, row, first):
+            for r in reversed(range(PACK)):
+                at = 2 * (first + r)
+                nc.tensor.transpose(area[:, at : at + P], row[:, r:N:PACK], ident[:])
+
+        def turned(area, count):
+            return area[:, ROW : ROW + 2 * count : 2]
+
+        kb_col = tile("kb_col", [P, B * PACK], F32)
+        for b in range(B):
+            turn_row(kb_bank[:, 0, :], kb_row[b], (B - 1 - b) * PACK)
+        nc.scalar.copy(kb_col[:], turned(kb_bank[:, 0, :], B * PACK))
+        turn_row(vs_turn[0], vs_row[0], 0)
         tail = [ps.tile([P, 2, P], F32, name="tail%d" % b) for b in range(B)]
 
-        k_pair = [tile("k_pair%d" % b, [P, N], U32) for b in range(B)]
         k_code = [tile("k_code%d" % b, [P, PASSES * N * 2], U8) for b in range(B)]
-        q_bf = [tile("q_bf%d" % b, [P, PASSES * NQ * PACK], BF16) for b in range(B)]
         q_code = [tile("q_code%d" % b, [P, PASSES * NQ], U32) for b in range(B)]
         q_scale = [tile("q_scale%d" % b, [P, PASSES * NQ], U8) for b in range(B)]
 
         def keys_and_scores(b):
+            k_pair = tile("k_pair%d" % b, [P, N], U32, tag="k_pair")
+            q_bf = tile("q_bf%d" % b, [P, PASSES * NQ * PACK], BF16)
             nc.vector.tensor_copy(
-                k_pair[b][:].rearrange("p (r s) -> p s r", r=PACK),
-                word_pool[:, 0 : (b + 1) * SEG].bitcast(U32).indirect(seq_offsets[b]),
+                k_pair[:].rearrange("p (r s) -> p s r", r=PACK),
+                word_pool[:].bitcast(U32).indirect(seq_offsets[b]),
             )
-            nc.gpsimd.tensor_scalar(
-                q_bf[b][:].rearrange("p (o q j) -> p o q j", o=PASSES, j=PACK),
-                q_raw[b][:].rearrange("p o j q -> p o q j"),
-                1.0,
-                0.0,
-                ALU.mult,
-                ALU.add,
+            interleave = nc.scalar.copy if b else nc.vector.tensor_copy
+            interleave(
+                q_bf[:].rearrange("p (o c i j) -> p o c j i", o=PASSES, i=4, j=PACK),
+                q_raw[b][:].rearrange("p o j (c i) -> p o c j i", i=4),
             )
             nc.vector.tensor_copy(
                 k_code[b][:].bitcast(U16).rearrange("p (o n) -> p o n", o=PASSES),
-                k_pair[b][:].bitcast(U16).rearrange("p (n o) -> p o n", o=PASSES),
+                k_pair[:].bitcast(U16).rearrange("p (n o) -> p o n", o=PASSES),
             )
-            nc.vector.quantize_mx(out=q_code[b][:].bitcast(FP8X4), scales=q_scale[b][:], in_=q_bf[b][:])
+            nc.vector.quantize_mx(out=q_code[b][:].bitcast(FP8X4), scales=q_scale[b][:], in_=q_bf[:])
             for r in range(PACK):
                 for o in range(PASSES):
                     at = (o * N + r * P) * 2
@@ -151,11 +160,8 @@ def tile_attend_rel2_kb_segb2q128n512t2048_kernel(tc, qT, k_words, k_scales, vT,
         v_scale = [tile("v_scale%d" % b, [P, DV], U8) for b in range(B)]
 
         def values(b):
-            v_slot = tile("v_slot%d" % b, [P, N], BF16, tag="relu0" if b else "")
-            if b == 0:
-                nc.vector.tensor_copy(v_slot[:], v_pool[b][:].indirect(seq_offsets[b]))
-            else:
-                nc.scalar.activation(v_slot[:], v_pool[b][:].indirect(seq_offsets[b]), ACT.Copy)
+            v_slot = tile("v_slot%d" % b, [P, N], BF16, tag="relu0")
+            nc.scalar.activation(v_slot[:], v_pool[:].indirect(seq_offsets[b]), ACT.Copy)
             pairs = v_slot[:].bitcast(F32)
             for u in range(2):
                 nc.tensor.transpose(v_turn[b][:, u, :], pairs[:, u : N // 2 : 2], ident[:])
@@ -178,18 +184,24 @@ def tile_attend_rel2_kb_segb2q128n512t2048_kernel(tc, qT, k_words, k_scales, vT,
         def positive_scores(b):
             last = b == B - 1
             for r in range(PACK):
-                score, bias = scores[b][r], kb_col[b][:, r : r + 1]
+                at = (B - 1 - b) * PACK + r
+                score, bias = scores[b][r], kb_col[:, at : at + 1]
                 if last:
                     nc.vector.tensor_scalar(relu[b][:, r, :], score, bias, 0.0, ALU.add, ALU.max)
                 else:
                     nc.scalar.activation(relu[b][:, r, :], score, ACT.Relu, bias=bias)
-            nc.scalar.activation(prob[b][:], relu[b][:], ACT.Square)
+            if last:
+                for h in range(2):
+                    pair = relu[b][:, 2 * h : 2 * h + 2, :]
+                    nc.vector.tensor_tensor(prob[b][:, 2 * h : 2 * h + 2, :], pair, pair, ALU.mult)
+            else:
+                nc.scalar.activation(prob[b][:], relu[b][:], ACT.Square)
 
         def weights(b):
             nc.vector.tensor_tensor(
                 w_bf[b][:].rearrange("p (q r) -> p q r", r=PACK),
                 prob[b][:].rearrange("p r q -> p q r"),
-                vs_col[b][:].unsqueeze(1).broadcast_to([P, NQ, PACK]),
+                turned(vs_turn[b], PACK).unsqueeze(1).broadcast_to([P, NQ, PACK]),
                 ALU.mult,
             )
             for r in range(PACK):
@@ -216,12 +228,12 @@ def tile_attend_rel2_kb_segb2q128n512t2048_kernel(tc, qT, k_words, k_scales, vT,
             nc.sync.dma_start(out[b], res[b][:])
 
         keys_and_scores(0)
-        nc.gpsimd.memset(v_pool[1][:, 0:SEG], 0.0)
         keys_and_scores(1)
         positive_scores(0)
+        turn_row(vs_turn[1], vs_row[1], 0)
         values(0)
-        positive_scores(1)
         weights(0)
+        positive_scores(1)
         values(1)
         finish(0)
         weights(1)

@@ -68,6 +68,8 @@ def tile_attend_rel2_kb_segb2q128n512t2048_kernel(tc, qT, k_words, k_scales, vT,
         nc.sync.dma_start(word_pool[:], words_hbm)
         nc.sync.dma_start(vs_pool[ROW:P, :], vs[0:1, :])
         load_queries(1)
+        v_pool = tile("v_pool", [P, T], F32)
+        nc.sync.dma_start(v_pool[:], vT)
 
         for rows in (slice(0, FREE), slice(32, 32 + FREE), slice(HALF, P)):
             nc.gpsimd.memset(scale_pool[rows, :].bitcast(I32), 0)
@@ -87,8 +89,6 @@ def tile_attend_rel2_kb_segb2q128n512t2048_kernel(tc, qT, k_words, k_scales, vT,
                     k_scale[h * HALF : (h + 1) * HALF, o * B * N : (o + 1) * B * N].bitcast(I32),
                     k_scale_slot[first : first + HALF, :].bitcast(I32),
                 )
-        v_pool = tile("v_pool", [P, T], F32, tag="scale_pool")
-        nc.sync.dma_start(v_pool[:], vT)
 
         def gather_row(name, pool, b):
             row = tile("%s_row%d" % (name, b), [P, N], F32)
@@ -102,7 +102,7 @@ def tile_attend_rel2_kb_segb2q128n512t2048_kernel(tc, qT, k_words, k_scales, vT,
         scores = [[banks[b][r // 2][:, 0, (r % 2) * NQ : (r % 2 + 1) * NQ] for r in range(PACK)] for b in range(B)]
         kb_bank = ps.tile([P, 2, 2 * P], F32, name="kb_bank")
         vs_bank = ps.tile([P, 2 * P], F32, name="vs_bank")
-        vs_turn = [vs_bank[:], banks[0][0][:, 1, :]]
+        vs_turn = [vs_bank[:], banks[1][0][:, 1, :]]
         v_turn = [area.rearrange("p (u e) -> p u e", u=2) for area in (banks[0][1][:, 1, :], kb_bank[:, 1, :])]
 
         def turn_row(area, row, first):
@@ -160,8 +160,11 @@ def tile_attend_rel2_kb_segb2q128n512t2048_kernel(tc, qT, k_words, k_scales, vT,
         v_scale = [tile("v_scale%d" % b, [P, DV], U8) for b in range(B)]
 
         def values(b):
-            v_slot = tile("v_slot%d" % b, [P, N], BF16, tag="relu0")
-            nc.scalar.activation(v_slot[:], v_pool[:].indirect(seq_offsets[b]), ACT.Copy)
+            v_slot = tile("v_slot%d" % b, [P, N], BF16)
+            if b == 0:
+                nc.vector.tensor_copy(v_slot[:], v_pool[:].indirect(seq_offsets[b]))
+            else:
+                nc.scalar.activation(v_slot[:], v_pool[:].indirect(seq_offsets[b]), ACT.Copy)
             pairs = v_slot[:].bitcast(F32)
             for u in range(2):
                 nc.tensor.transpose(v_turn[b][:, u, :], pairs[:, u : N // 2 : 2], ident[:])
@@ -186,14 +189,13 @@ def tile_attend_rel2_kb_segb2q128n512t2048_kernel(tc, qT, k_words, k_scales, vT,
             for r in range(PACK):
                 at = (B - 1 - b) * PACK + r
                 score, bias = scores[b][r], kb_col[:, at : at + 1]
-                if last:
+                if last and r < 2:
                     nc.vector.tensor_scalar(relu[b][:, r, :], score, bias, 0.0, ALU.add, ALU.max)
                 else:
                     nc.scalar.activation(relu[b][:, r, :], score, ACT.Relu, bias=bias)
             if last:
-                for h in range(2):
-                    pair = relu[b][:, 2 * h : 2 * h + 2, :]
-                    nc.vector.tensor_tensor(prob[b][:, 2 * h : 2 * h + 2, :], pair, pair, ALU.mult)
+                nc.vector.tensor_tensor(prob[b][:, 0:2, :], relu[b][:, 0:2, :], relu[b][:, 0:2, :], ALU.mult)
+                nc.scalar.activation(prob[b][:, 2:4, :], relu[b][:, 2:4, :], ACT.Square)
             else:
                 nc.scalar.activation(prob[b][:], relu[b][:], ACT.Square)
 
@@ -208,9 +210,7 @@ def tile_attend_rel2_kb_segb2q128n512t2048_kernel(tc, qT, k_words, k_scales, vT,
                 nc.tensor.matmul(
                     tail[b][:, 0, :], prob[b][:, r, :], ident[:], start=(r == 0), stop=(r == PACK - 1), is_transpose=True
                 )
-            nc.vector.tensor_scalar(
-                part[b][:], tail[b][:, 0, :], 1.0, 1.0, ALU.mult, ALU.add, accum_out=total[b][:]
-            )
+            nc.scalar.activation(part[b][:], tail[b][:, 0, :], ACT.Copy, bias=1.0 / P, accum_out=total[b][:])
             nc.vector.quantize_mx(out=w_code[b][:].bitcast(FP8X4), scales=w_scale[b][:], in_=w_bf[b][:])
             nc.vector.reciprocal(inv[b][:], total[b][:])
 
@@ -230,10 +230,10 @@ def tile_attend_rel2_kb_segb2q128n512t2048_kernel(tc, qT, k_words, k_scales, vT,
         keys_and_scores(0)
         keys_and_scores(1)
         positive_scores(0)
+        positive_scores(1)
         turn_row(vs_turn[1], vs_row[1], 0)
         values(0)
         weights(0)
-        positive_scores(1)
         values(1)
         finish(0)
         weights(1)

from contextlib import ExitStack

import concourse.mybir as mybir
from concourse.masks import make_identity

B, N, T, D, DV, NQ = 2, 512, 2048, 1024, 128, 128
SEG = T // B
P = 128
PACK = 4
PASSES = D // (P * PACK)

FLOPS = 2 * B * NQ * N * (D + DV)
BYTES = 4 * B * D * NQ + 4 * P * T + PASSES * 16 * T + 4 * DV * T + 2 * 4 * T + 2 * P * (B * N // 16) + 4 * B * NQ * DV

F32 = mybir.dt.float32
BF16 = mybir.dt.bfloat16
I32 = mybir.dt.int32
U32 = mybir.dt.uint32
U16 = mybir.dt.uint16
U8 = mybir.dt.uint8
FP8X4 = mybir.dt.float8_e4m3fn_x4
FP4X4 = mybir.dt.float4_e2m1fn_x4
ACT = mybir.ActivationFunctionType
ALU = mybir.AluOpType

ROW = P - 1
FREE = 16
HALF = P // 2


def tile_attend_rel2_kb_segb2q128n512t2048_kernel(tc, qT, k_words, k_scales, vT, vs, kb, offs, out):
    nc = tc.nc
    with ExitStack() as ctx:
        lists = ctx.enter_context(tc.tile_pool(name="lists", bufs=1))
        sb = ctx.enter_context(tc.tile_pool(name="sb", bufs=1))
        ps = ctx.enter_context(tc.psum_pool(name="ps", bufs=1))

        def tile(name, shape, dtype, tag=""):
            return sb.tile(shape, dtype, name=name, tag=tag or name, align_bytes=64)

        offsets = lists.tile([P, B * N // 16], U16, name="offsets")
        seq_offsets = [offsets[:, b * N // 16 : (b + 1) * N // 16] for b in range(B)]

        scale_pool = tile("scale_pool", [P, T], U8)
        kb_pool = tile("kb_pool", [P, T], F32)
        vs_pool = tile("vs_pool", [P, T], F32)
        word_pool = tile("word_pool", [P, T], I32)
        q_raw = [tile("q_raw%d" % b, [P, PASSES, PACK, NQ], F32) for b in range(B)]
        k_scale_slot = tile("k_scale_slot", [P, B * N], U8)
        k_scale = tile("k_scale", [P, PASSES * B * N], U8)
        ident = tile("ident", [P, P], F32)

        nc.sync.dma_start(offsets[:], offs)
        nc.sync.dma_start(kb_pool[ROW:P, :], kb[0:1, :])
        scale_rows = k_scales.rearrange("o (h c j) t -> c (o h) j t", h=2, c=2)
        for c in range(2):
            nc.sync.dma_start(
                scale_pool[32 * c + FREE : 32 * c + 32, :].bitcast(I32),
                scale_rows[c].bitcast(I32),
            )
        words_hbm = k_words[0].rearrange("p t c -> p (t c)").bitcast(I32)


        def load_queries(b):
            nc.sync.dma_start(q_raw[b][:], qT[b].rearrange("(o p j) q -> p o j q", o=PASSES, j=PACK))

        load_queries(0)
        nc.sync.dma_start(word_pool[:], words_hbm)
        nc.sync.dma_start(vs_pool[ROW:P, :], vs[0:1, :])
        load_queries(1)
        v_pool = tile("v_pool", [P, T], F32)
        nc.sync.dma_start(v_pool[:], vT)

        for rows in (slice(0, FREE), slice(32, 32 + FREE), slice(HALF, P)):
            nc.gpsimd.memset(scale_pool[rows, :].bitcast(I32), 0)
        nc.vector.memset(kb_pool[0:ROW, 0 : SEG - 1], 0.0)
        nc.vector.memset(kb_pool[0:ROW, SEG - 1 : T], 0.0)
        nc.gpsimd.memset(vs_pool[0:ROW, :], 0.0)
        make_identity(nc, ident[:])

        nc.vector.tensor_copy(
            k_scale_slot[:].rearrange("p (r n) -> p n r", r=PACK),
            scale_pool[:].indirect(offsets[:]),
        )
        for o in range(PASSES):
            for h in range(2):
                first = FREE + 4 * (2 * o + h)
                nc.sync.dma_start(
                    k_scale[h * HALF : (h + 1) * HALF, o * B * N : (o + 1) * B * N].bitcast(I32),
                    k_scale_slot[first : first + HALF, :].bitcast(I32),
                )

        def gather_row(name, pool, b):
            row = tile("%s_row%d" % (name, b), [P, N], F32)
            nc.scalar.activation(row[:], pool[:].indirect(seq_offsets[b]), ACT.Copy)
            return row

        kb_row = [gather_row("kb", kb_pool, b) for b in range(B)]
        vs_row = [gather_row("vs", vs_pool, b) for b in range(B)]

        banks = [[ps.tile([P, 2, 2 * P], F32, name="scores%d%d" % (b, h)) for h in range(2)] for b in range(B)]
        scores = [[banks[b][r // 2][:, 0, (r % 2) * NQ : (r % 2 + 1) * NQ] for r in range(PACK)] for b in range(B)]
        kb_bank = ps.tile([P, 2, 2 * P], F32, name="kb_bank")
        vs_bank = ps.tile([P, 2 * P], F32, name="vs_bank")
        vs_turn = [vs_bank[:], banks[1][0][:, 1, :]]
        v_turn = [area.rearrange("p (u e) -> p u e", u=2) for area in (banks[0][1][:, 1, :], kb_bank[:, 1, :])]

        def turn_row(area, row, first):
            for r in reversed(range(PACK)):
                at = 2 * (first + r)
                nc.tensor.transpose(area[:, at : at + P], row[:, r:N:PACK], ident[:])

        def turned(area, count):
            return area[:, ROW : ROW + 2 * count : 2]

        kb_col = tile("kb_col", [P, B * PACK], F32)
        for b in range(B):
            turn_row(kb_bank[:, 0, :], kb_row[b], (B - 1 - b) * PACK)
        nc.scalar.copy(kb_col[:], turned(kb_bank[:, 0, :], B * PACK))
        turn_row(vs_turn[0], vs_row[0], 0)
        tail = [ps.tile([P, 2, P], F32, name="tail%d" % b) for b in range(B)]

        k_code = [tile("k_code%d" % b, [P, PASSES * N * 2], U8) for b in range(B)]
        q_code = [tile("q_code%d" % b, [P, PASSES * NQ], U32) for b in range(B)]
        q_scale = [tile("q_scale%d" % b, [P, PASSES * NQ], U8) for b in range(B)]

        def keys_and_scores(b):
            k_pair = tile("k_pair%d" % b, [P, N], U32, tag="k_pair")
            q_bf = tile("q_bf%d" % b, [P, PASSES * NQ * PACK], BF16)
            nc.vector.tensor_copy(
                k_pair[:].rearrange("p (r s) -> p s r", r=PACK),
                word_pool[:].bitcast(U32).indirect(seq_offsets[b]),
            )
            interleave = nc.scalar.copy if b else nc.vector.tensor_copy
            interleave(
                q_bf[:].rearrange("p (o c i j) -> p o c j i", o=PASSES, i=4, j=PACK),
                q_raw[b][:].rearrange("p o j (c i) -> p o c j i", i=4),
            )
            nc.vector.tensor_copy(
                k_code[b][:].bitcast(U16).rearrange("p (o n) -> p o n", o=PASSES),
                k_pair[:].bitcast(U16).rearrange("p (n o) -> p o n", o=PASSES),
            )
            nc.vector.quantize_mx(out=q_code[b][:].bitcast(FP8X4), scales=q_scale[b][:], in_=q_bf[:])
            for r in range(PACK):
                for o in range(PASSES):
                    at = (o * N + r * P) * 2
                    col = o * B * N + (r * B + b) * P
                    nc.tensor.matmul_mx(
                        out=scores[b][r],
                        lhsT=k_code[b][:, at : at + 2 * P].bitcast(FP4X4),
                        lhsT_scale=k_scale[:, col : col + P],
                        rhs=q_code[b][:, o * NQ : (o + 1) * NQ].bitcast(FP8X4),
                        rhs_scale=q_scale[b][:, o * NQ : (o + 1) * NQ],
                        start=(o == 0),
                        stop=(o == PASSES - 1),
                    )

        v_bf = [tile("v_bf%d" % b, [P, DV * PACK], BF16) for b in range(B)]
        v_code = [tile("v_code%d" % b, [P, DV], U32) for b in range(B)]
        v_scale = [tile("v_scale%d" % b, [P, DV], U8) for b in range(B)]

        def values(b):
            v_slot = tile("v_slot%d" % b, [P, N], BF16)
            if b == 0:
                nc.vector.tensor_copy(v_slot[:], v_pool[:].indirect(seq_offsets[b]))
            else:
                nc.scalar.activation(v_slot[:], v_pool[:].indirect(seq_offsets[b]), ACT.Copy)
            pairs = v_slot[:].bitcast(F32)
            for u in range(2):
                nc.tensor.transpose(v_turn[b][:, u, :], pairs[:, u : N // 2 : 2], ident[:])
            nc.scalar.copy(
                v_bf[b][:].bitcast(F32).rearrange("p (e u) -> p e u", u=2),
                v_turn[b].rearrange("p u e -> p e u"),
            )
            nc.vector.quantize_mx(out=v_code[b][:].bitcast(FP8X4), scales=v_scale[b][:], in_=v_bf[b][:])

        relu = [tile("relu%d" % b, [P, PACK, NQ], F32) for b in range(B)]
        prob = [tile("prob%d" % b, [P, PACK, NQ], F32) for b in range(B)]
        w_bf = [tile("w_bf%d" % b, [P, NQ * PACK], BF16) for b in range(B)]
        w_code = [tile("w_code%d" % b, [P, NQ], U32) for b in range(B)]
        w_scale = [tile("w_scale%d" % b, [P, NQ], U8) for b in range(B)]
        part = [tile("part%d" % b, [P, P], F32) for b in range(B)]
        total = [tile("total%d" % b, [P, 1], F32) for b in range(B)]
        inv = [tile("inv%d" % b, [P, 1], F32) for b in range(B)]
        res = [tile("res%d" % b, [P, DV], F32) for b in range(B)]

        def positive_scores(b):
            last = b == B - 1
            for r in range(PACK):
                at = (B - 1 - b) * PACK + r
                score, bias = scores[b][r], kb_col[:, at : at + 1]
                if last and r < 2:
                    nc.vector.tensor_scalar(relu[b][:, r, :], score, bias, 0.0, ALU.add, ALU.max)
                else:
                    nc.scalar.activation(relu[b][:, r, :], score, ACT.Relu, bias=bias)
            if last:
                nc.vector.tensor_tensor(prob[b][:, 0:2, :], relu[b][:, 0:2, :], relu[b][:, 0:2, :], ALU.mult)
                nc.scalar.activation(prob[b][:, 2:4, :], relu[b][:, 2:4, :], ACT.Square)
            else:
                nc.scalar.activation(prob[b][:], relu[b][:], ACT.Square)

        def weights(b):
            nc.vector.tensor_tensor(
                w_bf[b][:].rearrange("p (q r) -> p q r", r=PACK),
                prob[b][:].rearrange("p r q -> p q r"),
                turned(vs_turn[b], PACK).unsqueeze(1).broadcast_to([P, NQ, PACK]),
                ALU.mult,
            )
            for r in range(PACK):
                nc.tensor.matmul(
                    tail[b][:, 0, :], prob[b][:, r, :], ident[:], start=(r == 0), stop=(r == PACK - 1), is_transpose=True
                )
            nc.scalar.activation(part[b][:], tail[b][:, 0, :], ACT.Copy, bias=1.0 / P, accum_out=total[b][:])
            nc.vector.quantize_mx(out=w_code[b][:].bitcast(FP8X4), scales=w_scale[b][:], in_=w_bf[b][:])
            nc.vector.reciprocal(inv[b][:], total[b][:])

        def finish(b):
            nc.tensor.matmul_mx(
                out=tail[b][:, 1, :],
                lhsT=w_code[b][:].bitcast(FP8X4),
                lhsT_scale=w_scale[b][:],
                rhs=v_code[b][:].bitcast(FP8X4),
                rhs_scale=v_scale[b][:],
                start=True,
                stop=True,
            )
            nc.scalar.activation(res[b][:], tail[b][:, 1, :], ACT.Copy, scale=inv[b][:])
            nc.sync.dma_start(out[b], res[b][:])

        keys_and_scores(0)
        keys_and_scores(1)
        positive_scores(0)
        positive_scores(1)
        turn_row(vs_turn[1], vs_row[1], 0)
        values(0)
        weights(0)
        values(1)
        finish(0)
        weights(1)
        finish(1)
